import numpy as np
CORES = [65,66,69,71,193,194,197,199,321,322,325,327,449,450,453,455]
N = 16
T, KB = 1024, 32
CAPP = 128
def entries(a): return a.T.reshape(-1)
def pack(v, P): return np.ascontiguousarray(np.asarray(v, np.int32).reshape(-1, P).T)
def order(K):
    return np.argsort(K, kind="stable")
def most(K):
    o = order(K); return int(np.bincount(o // T * N + np.arange(N * T) // T, minlength=N * N).max())
def lists(rng, how):
    i, G = np.arange(N), T // CAPP
    if how == "uniform":
        for again in range(50):
            K = rng.integers(0, KB, (N, T))
            if most(K.reshape(-1)) <= CAPP: break
        else: K = np.broadcast_to(np.arange(T) % KB, (N, T)).copy()
    else:
        if how == "uneven":
            t = rng.integers(0, CAPP + 1, N)
            if t.sum() < T: t = CAPP - t
            t[0] = CAPP; w = np.diff(np.minimum(np.cumsum(t), T), prepend=0); L = w[(rng.permutation(N)[:, None] - rng.permutation(N)) % N]
        else:
            w = np.zeros(N, int); w[(G * (ord(how[-1]) - 97) + np.arange(G)) % N] = CAPP; L = w[(i[:, None] - i) % N]
        a = N - 1 - np.argmax(L[::-1] > 0, axis=0)
        m = np.minimum(rng.integers(1, CAPP, N - 1), L[a[:-1], i[1:]])
        v = np.nonzero((L[a[:-1], i[:-1]] == CAPP) & (L[a[:-1], i[1:]] == CAPP) & (a[:-1] != np.append(-1, a[:-2])))[0]
        if len(v): m[rng.choice(v)] = CAPP
        C = L.copy(); C[a[:-1], i[:-1]] += m; C[a[:-1], i[1:]] -= m
        kv = np.sort(rng.permutation(KB)[:N]); K = np.stack([rng.permutation(np.repeat(kv, c)) for c in C]); K[::3] = np.sort(K[::3], axis=1)
    return {"key": np.stack([pack(k, 16) for k in K])}
def setup_inputs(rng):
    return dict({"x": rng.standard_normal((N, 128, T), dtype=np.float32)}, **lists(rng, "uniform"))
def setup_inputs_fulla(rng):
    d = setup_inputs(rng); d.update(lists(rng, "fulla"))
    for k in ("x",): d[k] = (d[k].astype(np.float32) * 1048576.0).astype(d[k].dtype)
    return d
def setup_inputs_fullb(rng):
    d = setup_inputs(rng); d.update(lists(rng, "fullb"))
    for k in ("x",): d[k] = (d[k].astype(np.float32) * (1 / 1024.0)).astype(d[k].dtype)
    return d
def setup_inputs_uneven(rng):
    d = setup_inputs(rng); d.update(lists(rng, "uneven"))
    return d
def check_inputs(x):
    bad = []
    if x["key"].min() < 0 or x["key"].max() >= KB: bad.append("key out of range")
    if most(np.concatenate([entries(a) for a in x["key"]])) > CAPP: bad.append("more than CAPP columns go from one rank to one rank")
    return bad
def reference(x, key):
    X = np.concatenate(list(x), axis=1); K = np.concatenate([entries(a) for a in key])
    Y = X[:, order(K)]
    return {"y": np.stack([Y[:, T * r:T * r + T] for r in range(N)])}

@@ -1,0 +1,357 @@
+from concourse.bass import DstId, RemoteDMATransfer
+from concourse.mybir import AluOpType as Op
+
+N, TC, CAP = 16, 1024, 128
+
+SCRATCH = {
+    "xs": ("sbuf", [128, TC], "float32"),
+    "xp": ("sbuf", [128, TC + CAP], "float32"),
+    "snd": ("sbuf", [128, N * CAP], "float32"),
+    "land": ("sbuf", [128, N * CAP], "float32"),
+    "rela": ("sbuf", [128, 2 * CAP], "float32"),
+    "relb": ("sbuf", [128, 2 * CAP], "float32"),
+    "yb": ("sbuf", [128, TC], "float32"),
+    "cland": ("dram", [N, 128, 1], "float32"),
+    "keyr": ("sbuf", [128, 64], "int32"),
+    "pi": ("sbuf", [128, 2], "int32"),
+    "fi": ("sbuf", [128, 128], "int32"),
+    "fb": ("sbuf", [128, 384], "int32"),
+    "kk": ("sbuf", [128, 16], "float32"),
+    "pci": ("sbuf", [128, 8], "int32"),
+    "pcf": ("sbuf", [128, 8], "float32"),
+    "onesb": ("sbuf", [128, 264], "bfloat16"),
+    "eq": ("sbuf", [128, 264], "bfloat16"),
+    "acc": ("sbuf", [128, 264], "bfloat16"),
+    "sl8": ("sbuf", [128, 16], "bfloat16"),
+    "msg": ("sbuf", [128, 8], "float32"),
+    "zmsg": ("sbuf", [128, 4], "float32"),
+    "wsame": ("sbuf", [128, 128], "bfloat16"),
+    "wle": ("sbuf", [128, 128], "bfloat16"),
+    "wneg": ("sbuf", [128, 128], "bfloat16"),
+    "wlt": ("sbuf", [128, 128], "bfloat16"),
+    "selq": ("sbuf", [128, 128], "float32"),
+    "rb": ("sbuf", [128, 256], "float32"),
+    "rbe": ("sbuf", [128, 256], "float32"),
+    "off1": ("sbuf", [128, 64], "uint16"),
+    "selb": ("sbuf", [128, 128], "bfloat16"),
+    "lc": ("sbuf", [128, 128], "bfloat16"),
+    "d8": ("sbuf", [128, 128], "float32"),
+    "z48": ("sbuf", [128, 48], "float32"),
+    "wb": ("sbuf", [128, 48], "float32"),
+    "wi": ("sbuf", [128, 48], "float32"),
+    "cb": ("sbuf", [128, 64], "float32"),
+    "c1": ("sbuf", [128, 128], "float32"),
+    "c2": ("sbuf", [128, 128], "bfloat16"),
+    "off2": ("sbuf", [128, 128], "uint16"),
+    "bk": ("sbuf", [128, 512], "bfloat16"),
+    "zz": ("sbuf", [128, 8], "bfloat16"),
+    "ti": ("sbuf", [128, 12], "int32"),
+    "tf": ("sbuf", [128, 32], "float32"),
+    "qf": ("sbuf", [128, 128], "float32"),
+    "cf": ("sbuf", [128, 64], "float32"),
+    "cq": ("sbuf", [128, 64], "float32"),
+    "ci": ("sbuf", [128, 64], "float32"),
+    "onef": ("sbuf", [128, 128], "float32"),
+    "lm": ("sbuf", [128, 512], "float32"),
+    "r1": ("sbuf", [128, 256], "float32"),
+    "r2": ("sbuf", [128, 256], "float32"),
+    "w1": ("sbuf", [128, 64], "float32"),
+    "off3": ("sbuf", [128, 64], "uint16"),
+}
+for _k in range(8):
+    SCRATCH["ps%d" % _k] = ("psum", [128, 512], "float32")
+
+SEMAPHORES = ["v", "t", "p",
+              "kd", "xd", "md", "zd", "cd", "yd",
+              "cnt", "rcv", "ra", "rb", "dat",
+              "ls"]
+
+
+def rank_program(g, core, T, topo):
+    rank = T.rank_of(core)
+    if rank is None:
+        return
+    V, PE, SY, SC = g.vector, g.tensor, g.sync, g.scalar
+    queue = {"v": V, "t": PE, "p": g, "y": SY, "s": SC}
+    made, known = {"v": 0, "t": 0, "p": 0}, {}
+
+    def need(qn, *toks):
+        most = {}
+        for s, n in toks:
+            most[s] = max(n, most.get(s, 0))
+        for s in most:
+            if known.get((qn, s), 0) < most[s]:
+                queue[qn].wait_ge(T.sem[s], most[s])
+                known[(qn, s)] = most[s]
+
+    def done(qn, ins):
+        made[qn] += 1
+        ins.then_inc(T.sem[qn], 1)
+        return (qn, made[qn])
+
+    cores = list(T.cores)
+    place = lambda c: (topo.host(c), topo.chip(c))
+    chipmates = [c for c in cores if c != core and place(c) == place(core)]
+    rackp = [c for c in cores if topo.same_plane(core, c)]
+    cabp = [c for c in cores if topo.may_write(core, c) and topo.rack(topo.host(c)) != topo.rack(topo.host(core))]
+    diag = [c for c in cores if c != core and not topo.may_write(core, c)]
+    lane = sorted(chipmates + [core]).index(core)
+    rpeer, cpeer = rackp[lane], cabp[lane]
+    rk = T.rank_of
+
+    def engines(dst):
+        m, e, out = topo.mask(core, dst), 0, []
+        while m >> e:
+            if (m >> e) & 1:
+                out.append(e)
+            e += 1
+        return out
+
+    off = [e for e in engines(rpeer) if e in engines(cpeer)]
+    rest = [e for e in engines(chipmates[0]) if e not in off]
+
+    def mask(es):
+        return sum(1 << e for e in es)
+
+    def dst(c):
+        rid, pid = topo.addr(c, core)
+        return DstId(rid=rid, pnc=pid)
+
+    left = [0]
+
+    def send(items):
+        ts = []
+        for to, es, sem, src, out in items:
+            ts.append(RemoteDMATransfer(dst_ids=[dst(c) for c in to], dma_engine_mask=mask(es), remote_sem=T.sem[sem],
+                                        srcs=[src], dsts=[out for c in to]))
+            left[0] += len(es)
+        g.remote_dma_fused(ts, local_sem=T.sem["ls"])
+
+    for j in range(8):
+        (SY if j % 2 == 0 else SC).dma_start(T.keyr[16 * j:16 * j + 16, :], T.key[:]).then_inc(T.sem["kd"], 16)
+    SC.dma_start(T.xs[:], T.x[:]).then_inc(T.sem["xd"], 16)
+    KD, XD = ("kd", 128), ("xd", 16)
+
+    g_pi = done("p", g.iota(T.pi[:], [[32, 2]], 0, 1))
+    g_m4 = done("p", g.iota(T.kk[:, 0:4], [[1, 4]], 0, 0, allow_small_or_imprecise_dtypes=True))
+    g_fi = done("p", g.iota(T.fi[:], [[1, 128]], 0, 0))
+    g_lc = done("p", g.iota(T.lc[0:16, :], [[0, 16], [16, 8]], 0, 1, allow_small_or_imprecise_dtypes=True))
+    g_d8 = done("p", g.iota(T.d8[0:32, :], [[TC, 16], [0, 8]], 0, 0, allow_small_or_imprecise_dtypes=True))
+
+    done("v", V.memset(T.onesb[:], 1.0))
+    done("v", V.memset(T.eq[:, 256:264], 0.0))
+    done("v", V.memset(T.acc[:, 0:1], 0.0))
+    v_zm = done("v", V.memset(T.zmsg[:], 0.0))
+    v_z48 = done("v", V.memset(T.z48[:], 0.0))
+    need("v", g_pi, g_m4)
+    done("v", V.tensor_scalar(T.pci[:, 0:1], T.pi[:, 0:1], 4, None, Op.arith_shift_right))
+    done("v", V.tensor_scalar(T.pci[:, 1:2], T.pi[:, 0:1], 15, None, Op.bitwise_and))
+    done("v", V.tensor_scalar(T.pci[:, 2:3], T.pi[:, 0:1], 5, None, Op.arith_shift_right))
+    done("v", V.tensor_scalar(T.pci[:, 3:4], T.pi[:, 1:2], 5, 3, Op.arith_shift_right, Op.bitwise_and))
+    need("v", done("v", V.tensor_copy(T.pci[:, 4:5], T.pi[:, 0:1])))
+    need("v", done("v", V.tensor_copy(T.pcf[:, 0:5], T.pci[:, 0:5])))
+    P16, P15, P32, P32n, P0 = (T.pcf[:, j:j + 1] for j in range(5))
+    need("v", done("v", V.tensor_scalar(T.kk[:, 4:5], P16, 4.0, None, Op.mult)))
+    v_kc = done("v", V.tensor_scalar(T.kk[:, 8:12], T.kk[:, 0:4], T.kk[:, 4:5], None, Op.add))
+    need("v", g_fi)
+    done("v", V.tensor_scalar(T.sl8[:, 0:8], T.fi[:, 0:8], P16, None, Op.is_equal))
+    v_l8 = done("v", V.tensor_scalar(T.sl8[:, 8:16], T.fi[:, 0:8], P16, None, Op.is_gt))
+
+    need("s", v_zm)
+    SC.dma_start(T.cland[rank, 64:128, :], T.zmsg[0:16, :]).then_inc(T.sem["zd"], 16)
+
+    need("v", KD, v_kc)
+    for m in range(4):
+        v_eq = done("v", V.tensor_scalar(T.eq[:, 64 * m:64 * m + 64], T.keyr[:], T.kk[:, 8 + m:9 + m], None, Op.is_equal))
+    need("v", v_eq)
+    v_ac = done("v", V.tensor_tensor_scan(T.acc[:, 1:261], T.onesb[:, 0:260], T.eq[:, 0:260], 0.0, Op.mult, Op.add))
+    need("t", v_ac, v_l8)
+    PE.matmul(T.ps0[0:8, 0:5], T.sl8[:, 8:16], T.acc[:, 256:261], True, False)
+    t_ms = done("t", PE.matmul(T.ps0[0:8, 0:5], T.sl8[:, 0:8], T.acc[:, 0:257:64], False, True))
+    need("v", t_ms)
+    v_ms = done("v", V.tensor_copy(T.msg[0:8, 0:5], T.ps0[0:8, 0:5]))
+    need("y", v_ms)
+    SY.dma_start(T.cland[rank, 0:32, :], T.msg[0:8, 0:4]).then_inc(T.sem["md"], 16)
+    need("s", v_ms)
+    SC.dma_start(T.cland[rank, 32:64, :], T.msg[0:8, 1:5]).then_inc(T.sem["md"], 16)
+    MD, ZD = ("md", 32), ("zd", 16)
+
+    def chain(tile, start, steps):
+        tok, src = start, T.z48
+        for op, fill, base, cm, sr, st in steps:
+            need("p", tok)
+            tok = done("p", g.affine_select(tile[0:N, :], src[0:N, :], [[4 * sr, 4], [st, 3], [sr, 4]], op, fill, base, cm))
+            src = tile
+        return tok
+    K = 1000
+    g_wb = chain(T.wb, v_z48, [(Op.is_gt, 1.0, 0, -1, 1, K),
+                               (Op.not_equal, -1.0, -K, 1, -1, K),
+                               (Op.not_equal, 1.0, -2 * K, 1, -1, K),
+                               (Op.not_equal, -1.0, 15 + 2 * K, -1, 100, -K)])
+    g_wi = chain(T.wi, v_z48, [(Op.is_ge, 1.0, 0, 1, -1, K),
+                               (Op.not_equal, 1.0, -K, 1, -1, K),
+                               (Op.not_equal, -1.0, 1 - 2 * K, 1, -1, K)])
+
+    own = T.cland[rank]
+    need("p", MD, ZD)
+    send([([rpeer], off[0:1], "rcv", own, own),
+          ([c for c in cabp + rackp if c != rpeer], off[1:2], "cnt", own, own)])
+    spread = (off[2:] + rest)[:12]
+    send([(chipmates[j:j + 1], spread[4 * j:4 * j + 4], "cnt", own, own) for j in range(3)])
+    RCV = ("rcv", 1)
+    need("p", RCV)
+    peer = T.cland[rk(rpeer)]
+    send([(cabp, off[0:1], "cnt", peer, peer)])
+    CNT = ("cnt", 3 * 4 + 7 + 4)
+
+    need("y", MD, RCV, CNT)
+    SY.dma_start(T.cb[0:N, :], T.cland[:, 0:64, :]).then_inc(T.sem["cd"], 16)
+    CD = ("cd", 16)
+
+    F16, F15, F32 = (T.fb[:, 128 * j:128 * j + 128] for j in range(3))
+    v_f16 = done("v", V.tensor_scalar(F16, T.fi[:], 4, None, Op.arith_shift_right))
+    v_f15 = done("v", V.tensor_scalar(F15, T.fi[:], 15, None, Op.bitwise_and))
+    v_wle = done("v", V.tensor_scalar(T.wle[:], T.fi[:], P0, -1.0, Op.is_le, Op.mult))
+    need("v", v_f16)
+    v_ws = done("v", V.tensor_scalar(T.wsame[:], F16, P16, None, Op.is_equal))
+    v_wl = done("v", V.tensor_scalar(T.wlt[:], F16, P16, None, Op.is_gt))
+    need("v", v_f15)
+    done("v", V.tensor_scalar(T.selq[:], F15, P15, None, Op.is_equal))
+    v_sb = done("v", V.tensor_scalar(T.selb[:], F15, P15, None, Op.is_equal))
+    need("v", v_ws, v_wle)
+    v_wn = done("v", V.tensor_tensor(T.wneg[:], T.wle[:], T.wsame[:], Op.mult))
+    need("t", v_wl)
+    t_b = done("t", PE.matmul(T.ps2[:, 0:1], T.wlt[:], T.acc[:, 256:257], True, True))
+    need("t", v_wn)
+    PE.matmul(T.ps1[:, 0:256], T.wsame[:], T.acc[:, 1:257], True, False)
+    t_r = done("t", PE.matmul(T.ps1[:, 0:256], T.wneg[:], T.eq[:, 0:256], False, True))
+    need("t", v_sb, g_lc)
+    PE.matmul(T.ps5[:, 0:128], T.selb[0:16, :], T.lc[0:16, :], True, False)
+    need("v", t_r, t_b)
+    need("v", done("v", V.tensor_scalar(T.rb[:], T.ps1[:, 0:256], T.ps2[:, 0:1], None, Op.add)))
+    v_re = done("v", V.tensor_tensor(T.rbe[:], T.rb[:], T.eq[:, 0:256], Op.mult))
+    need("t", v_re)
+    for m in range(4):
+        ins = PE.matmul(T.ps3[:, 0:64], T.selq[:], T.rbe[:, 64 * m:64 * m + 64], m == 0, m == 3)
+    t_p = done("t", ins)
+    v_xz = done("v", V.memset(T.xp[:, TC:], 0.0))
+    need("v", t_p)
+    need("v", done("v", V.tensor_copy(T.off1[:], T.ps3[:, 0:64])), XD)
+    v_xp = done("v", V.tensor_copy(T.xp[:, 0:TC].indirect(T.off1[:]), T.xs[:]))
+
+    HIF, LOF, DD = 0, 4, 8
+    U4, V4, BD, JC, O4 = (T.tf[:, j:j + 4] for j in (12, 16, 20, 24, 28))
+    BLK, NBLK, BLKS, BLK3 = (T.bk[:, 128 * j:128 * j + 128] for j in range(4))
+    g_cf = done("p", g.iota(T.cf[:], [[1, 64]], 0, 0, allow_small_or_imprecise_dtypes=True))
+    g_cq = done("p", g.iota(T.cq[:], [[16, 64]], TC * rank + CAP * (N - 1), 0, allow_small_or_imprecise_dtypes=True))
+    v_o4 = done("v", V.memset(O4, float(CAP)))
+    need("p", v_o4)
+    g_jc = done("p", g.affine_select(JC, O4, [[1000, 4]], Op.is_gt, float(-CAP * (N - 1)), -31, 1))
+    v_of = done("v", V.memset(T.onef[:], 1.0))
+    v_zz = done("v", V.memset(T.zz[:], 0.0))
+    v_qf = done("v", V.tensor_copy(T.qf[:], F15))
+    need("v", done("v", V.tensor_scalar(F32, T.fi[:], 5, None, Op.arith_shift_right)))
+    done("v", V.tensor_scalar(BLK, F32, P32, None, Op.is_equal))
+    done("v", V.tensor_scalar(NBLK, F32, P32, -1.0, Op.is_equal, Op.mult))
+    done("v", V.tensor_scalar(BLKS, F32, P32n, None, Op.is_equal))
+    need("v", v_of, done("v", V.tensor_scalar(T.kk[:, 5:6], P32, 3.0, -1.0, Op.is_equal, Op.mult)))
+    v_b3 = done("v", V.tensor_scalar(BLK3, T.onef[:], T.kk[:, 5:6], None, Op.mult))
+    need("v", g_cq)
+    v_ci = done("v", V.tensor_scalar(T.ci[:], T.cq[:], P15, None, Op.add))
+
+    q0, m0 = rank // 4, rank % 4
+    need("t", CD, g_wb, g_wi)
+    PE.matmul(T.ps4[0:32, 0:12], T.cb[0:N, 0:32], T.wb[0:N, 12 * q0:12 * q0 + 12], True, False)
+    t_s = done("t", PE.matmul(T.ps4[0:32, 0:12], T.cb[0:N, 32:64], T.wi[0:N, 12 * q0:12 * q0 + 12], False, True))
+    need("v", t_s, g_d8)
+    v_c1 = done("v", V.tensor_scalar(T.c1[0:32, :], T.d8[0:32, :], T.ps4[0:32, m0:m0 + 1], 0.0, Op.subtract, Op.max))
+    need("v", v_c1)
+    v_c2 = done("v", V.tensor_scalar(T.c2[0:32, :], T.c1[0:32, :], T.ps4[0:32, 4 + m0:5 + m0], None, Op.min))
+    need("t", v_c2)
+    t_l = done("t", PE.matmul(T.ps5[:, 0:128], T.onesb[0:32, 0:128], T.c2[0:32, :], False, True))
+    need("v", t_l)
+    v_o2 = done("v", V.tensor_copy(T.off2[:], T.ps5[:, 0:128]))
+
+    def gather(buf, lo, hi):
+        return done("v", V.tensor_copy(buf[:, CAP * lo:CAP * hi], T.xp[:].indirect(T.off2[:, 8 * lo:8 * hi])))
+
+    def cols(r, n=1):
+        return slice(CAP * r, CAP * (r + n))
+
+    need("v", v_o2, v_xp, v_xz)
+    dr = rk(diag[0])
+    tok = gather(T.snd, dr, dr + 4)
+    need("p", tok)
+    send([([rpeer], off[0::2], "rb", T.snd[:, cols(dr + 2, 2)], T.relb[:]),
+          ([cpeer], off[1::2], "ra", T.snd[:, cols(dr, 2)], T.rela[:])])
+    for grp in (rackp, cabp):
+        tok = gather(T.snd, rk(grp[0]), rk(grp[0]) + 4)
+    first = rank - lane
+    if lane:
+        tok = gather(T.snd, first, rank)
+    if lane < 3:
+        tok = gather(T.snd, rank + 1, first + 4)
+    v_own = gather(T.land, rank, rank + 1)
+    need("p", tok)
+    mine = T.land[:, cols(rank)]
+    items = []
+    for j in range(4):
+        items.append(([rackp[j]], off[2 * j:2 * j + 1], "dat", T.snd[:, cols(rk(rackp[j]))], mine))
+        items.append(([cabp[j]], off[2 * j + 1:2 * j + 2], "dat", T.snd[:, cols(rk(cabp[j]))], mine))
+    for j in range(3):
+        items.append(([chipmates[j]], rest[2 * j:2 * j + 2], "dat", T.snd[:, cols(rk(chipmates[j]))], mine))
+    send(items)
+    need("p", ("rb", 4), ("ra", 4))
+    items = []
+    for j in range(2):
+        items.append(([rackp[j]], off[4 * j:4 * j + 4:2], "dat", T.rela[:, cols(j)], T.land[:, cols(rk(cpeer))]))
+        items.append(([cabp[2 + j]], off[4 * j + 1:4 * j + 4:2], "dat", T.relb[:, cols(j)], T.land[:, cols(rk(rpeer))]))
+    send(items)
+    DAT = ("dat", 8 + 3 * 2 + 4 * 2)
+
+    for q in range(4):
+        o, w = T.ps6[32 * q:32 * q + 32, 0:12], slice(12 * q, 12 * q + 12)
+        PE.matmul(o, T.cb[0:N, 0:32], T.wb[0:N, w], True, False)
+        t_y = done("t", PE.matmul(o, T.cb[0:N, 32:64], T.wi[0:N, w], False, True))
+    need("v", t_y, g_jc)
+    v_ti = done("v", V.tensor_scalar(T.ti[:, 0:4], T.ps6[:, 0:4], float(TC * rank), None, Op.subtract))
+    v_u = done("v", V.tensor_scalar(U4, T.ps6[:, 0:4], -1.0, float(TC * rank), Op.mult, Op.add))
+    v_bd = done("v", V.tensor_tensor(BD, T.ps6[:, 8:12], JC, Op.add))
+    need("v", v_u)
+    need("v", done("v", V.tensor_scalar(V4, U4, 0.0, None, Op.max)), v_zz)
+    v_z = done("v", V.tensor_tensor(T.zz[:, 1:5], V4, T.ps6[:, 4:8], Op.min))
+    need("t", v_z, v_b3)
+    PE.matmul(T.ps7[:, 0:4], NBLK, T.zz[:, 1:5], True, False)
+    PE.matmul(T.ps7[:, 0:4], BLK, T.zz[:, 0:4], False, False)
+    t_d = done("t", PE.matmul(T.ps7[:, 0:4], BLKS, T.zz[:, 4:8], False, True))
+    t_15 = done("t", PE.matmul(T.ps2[:, 0:1], BLK3, T.zz[:, 4:5], True, True))
+    need("v", v_ti)
+    done("v", V.tensor_scalar(T.ti[:, 4:8], T.ti[:, 0:4], 4, None, Op.arith_shift_right))
+    need("v", done("v", V.tensor_scalar(T.ti[:, 8:12], T.ti[:, 0:4], 15, None, Op.bitwise_and)))
+    done("v", V.tensor_copy(T.tf[:, HIF:HIF + 8], T.ti[:, 4:12]))
+    need("v", t_d, v_bd)
+    v_dd = done("v", V.tensor_tensor(T.tf[:, DD:DD + 4], T.ps7[:, 0:4], BD, Op.add))
+    need("v", v_dd, v_qf, g_cf)
+    for m in range(4):
+        hi, lo, jump = (T.tf[:, b + m:b + m + 1] for b in (HIF, LOF, DD))
+        lm, r1, r2 = T.lm[:, 128 * m:128 * m + 128], T.r1[:, 64 * m:64 * m + 64], T.r2[:, 64 * m:64 * m + 64]
+        done("v", V.tensor_scalar(lm, T.qf[:], lo, None, Op.is_ge))
+        done("v", V.tensor_scalar(r1, T.cf[:], hi, jump, Op.is_equal, Op.mult))
+        need("t", done("v", V.tensor_scalar(r2, T.cf[:], hi, jump, Op.is_gt, Op.mult)))
+        PE.matmul(T.ps1[:, 0:64], lm, r1, m == 0, False)
+        ins = PE.matmul(T.ps1[:, 0:64], T.onef[:], r2, False, m == 3)
+    t_w = done("t", ins)
+    need("v", t_w, v_ci)
+    need("v", done("v", V.tensor_tensor(T.w1[:], T.ps1[:, 0:64], T.ci[:], Op.add)), t_15)
+    v_o3 = done("v", V.tensor_scalar(T.off3[:], T.w1[:], T.ps2[:, 0:1], None, Op.add))
+
+    need("v", v_o3, v_own, DAT)
+    for j in range(4):
+        w = slice(256 * j, 256 * j + 256)
+        tok = done("v", V.tensor_copy(T.yb[:, w], T.land[:].indirect(T.off3[:, 16 * j:16 * j + 16])))
+        qn = "ys"[j % 2]
+        need(qn, tok)
+        queue[qn].dma_start(T.y[:, w], T.yb[:, w]).then_inc(T.sem["yd"], 16)
+
+    need("p", ("ls", left[0]))
+    need("y", ("v", made["v"]), ("t", made["t"]), ("p", made["p"]), KD, XD, MD, ZD, CD, ("yd", 64))

@@ -1,5 +1,5 @@
 from concourse.bass import DstId, RemoteDMATransfer
-from concourse.mybir import AluOpType as Op
+from concourse.mybir import AluOpType as Op, ActivationFunctionType as Fn
 
 N, TC, CAP = 16, 1024, 128
 
@@ -8,8 +8,8 @@ SCRATCH = {
     "xp": ("sbuf", [128, TC + CAP], "float32"),
     "snd": ("sbuf", [128, N * CAP], "float32"),
     "land": ("sbuf", [128, N * CAP], "float32"),
-    "rela": ("sbuf", [128, 2 * CAP], "float32"),
-    "relb": ("sbuf", [128, 2 * CAP], "float32"),
+    "rela": ("sbuf", [128, CAP], "float32"),
+    "relb": ("sbuf", [128, CAP], "float32"),
     "yb": ("sbuf", [128, TC], "float32"),
     "cland": ("dram", [N, 128, 1], "float32"),
     "keyr": ("sbuf", [128, 64], "int32"),
@@ -61,19 +61,42 @@ SCRATCH = {
 for _k in range(8):
     SCRATCH["ps%d" % _k] = ("psum", [128, 512], "float32")
 
-SEMAPHORES = ["v", "t", "p",
-              "kd", "xd", "md", "zd", "cd", "yd",
+SEMAPHORES = ["v", "t", "p", "s",
+              "kd", "xd",
+              "md", "zd", "cd", "yd",
               "cnt", "rcv", "ra", "rb", "dat",
               "ls"]
+HELPER, RELAY = {}, {}
+
+
+def plan(cores, topo):
+    if HELPER:
+        return
+    world = range(512)
+    spot = lambda k: (topo.host(k), topo.chip(k))
+    for c in cores:
+        side = [k for k in world if spot(k) == spot(c) and topo.die(k) == topo.die(c)]
+        idle = [k for k in side if k not in cores]
+        HELPER[c] = idle[[k for k in side if k in cores].index(c)]
+        here = [k for k in world if spot(k) == spot(c)].index(c)
+        others = sorted({topo.chip(k) for k in world if topo.host(k) == topo.host(c) and topo.same_plane(k, c)})
+        RELAY[c] = [[k for k in world if spot(k) == (topo.host(c), e)][here] for e in others[:4]]
 
 
 def rank_program(g, core, T, topo):
-    rank = T.rank_of(core)
-    if rank is None:
+    place = lambda c: (topo.host(c), topo.chip(c))
+    cores = list(T.cores)
+    plan(cores, topo)
+    base = None
+    for c in cores:
+        if core in (c, HELPER[c]) or core in RELAY[c]:
+            base = c
+    if base is None:
         return
+    rank, isr = T.rank_of(base), core == base
     V, PE, SY, SC = g.vector, g.tensor, g.sync, g.scalar
     queue = {"v": V, "t": PE, "p": g, "y": SY, "s": SC}
-    made, known = {"v": 0, "t": 0, "p": 0}, {}
+    made, known = {"v": 0, "t": 0, "p": 0, "s": 0}, {}
 
     def need(qn, *toks):
         most = {}
@@ -89,15 +112,15 @@ def rank_program(g, core, T, topo):
         ins.then_inc(T.sem[qn], 1)
         return (qn, made[qn])
 
-    cores = list(T.cores)
-    place = lambda c: (topo.host(c), topo.chip(c))
-    chipmates = [c for c in cores if c != core and place(c) == place(core)]
-    rackp = [c for c in cores if topo.same_plane(core, c)]
-    cabp = [c for c in cores if topo.may_write(core, c) and topo.rack(topo.host(c)) != topo.rack(topo.host(core))]
-    diag = [c for c in cores if c != core and not topo.may_write(core, c)]
-    lane = sorted(chipmates + [core]).index(core)
+    chipmates = [c for c in cores if c != base and place(c) == place(base)]
+    chip4 = sorted(chipmates + [base])
+    rackp = [c for c in cores if topo.same_plane(base, c)]
+    cabp = [c for c in cores if topo.may_write(base, c) and topo.rack(topo.host(c)) != topo.rack(topo.host(base))]
+    diag = [c for c in cores if c != base and not topo.may_write(base, c)]
+    lane = chip4.index(base)
     rpeer, cpeer = rackp[lane], cabp[lane]
     rk = T.rank_of
+    hof = lambda cs: [HELPER[c] for c in cs]
 
     def engines(dst):
         m, e, out = topo.mask(core, dst), 0, []
@@ -127,22 +150,41 @@ def rank_program(g, core, T, topo):
             left[0] += len(es)
         g.remote_dma_fused(ts, local_sem=T.sem["ls"])
 
-    for j in range(8):
-        (SY if j % 2 == 0 else SC).dma_start(T.keyr[16 * j:16 * j + 16, :], T.key[:]).then_inc(T.sem["kd"], 16)
-    SC.dma_start(T.xs[:], T.x[:]).then_inc(T.sem["xd"], 16)
-    KD, XD = ("kd", 128), ("xd", 16)
+    def cols(r, n=1):
+        return slice(CAP * r, CAP * (r + n))
+
+    if core in RELAY[base]:
+        j = RELAY[base].index(core)
+        need("p", ("ra", 1))
+        send([([RELAY[cpeer][j]], off, "rb", T.rela[:], T.relb[:])])
+        need("p", ("rb", len(off)))
+        send([([chip4[j]], off, "dat", T.relb[:], T.land[:, cols(rk(diag[lane]))])])
+        need("p", ("ls", left[0]))
+        return
+
+    if isr:
+        for j in range(8):
+            (SY if j % 2 == 0 else SC).dma_start(T.keyr[16 * j:16 * j + 16, :], T.key[:]).then_inc(T.sem["kd"], 16)
+        SC.dma_start(T.xs[:], T.x[:]).then_inc(T.sem["xd"], 16)
+    KD, XD = (("kd", 128), ("xd", 16)) if isr else (("kd", len(off)), ("xd", len(rest)))
 
     g_pi = done("p", g.iota(T.pi[:], [[32, 2]], 0, 1))
     g_m4 = done("p", g.iota(T.kk[:, 0:4], [[1, 4]], 0, 0, allow_small_or_imprecise_dtypes=True))
     g_fi = done("p", g.iota(T.fi[:], [[1, 128]], 0, 0))
     g_lc = done("p", g.iota(T.lc[0:16, :], [[0, 16], [16, 8]], 0, 1, allow_small_or_imprecise_dtypes=True))
     g_d8 = done("p", g.iota(T.d8[0:32, :], [[TC, 16], [0, 8]], 0, 0, allow_small_or_imprecise_dtypes=True))
+    if isr:
+        g_cf = done("p", g.iota(T.cf[:], [[1, 64]], 0, 0, allow_small_or_imprecise_dtypes=True))
+        g_cq = done("p", g.iota(T.cq[:], [[16, 64]], TC * rank + CAP * (N - 1), 0, allow_small_or_imprecise_dtypes=True))
+        need("p", KD)
+        send([([HELPER[core]], off, "kd", T.keyr[:], T.keyr[:])])
 
     done("v", V.memset(T.onesb[:], 1.0))
     done("v", V.memset(T.eq[:, 256:264], 0.0))
     done("v", V.memset(T.acc[:, 0:1], 0.0))
-    v_zm = done("v", V.memset(T.zmsg[:], 0.0))
     v_z48 = done("v", V.memset(T.z48[:], 0.0))
+    if isr:
+        v_zm = done("v", V.memset(T.zmsg[:], 0.0))
     need("v", g_pi, g_m4)
     done("v", V.tensor_scalar(T.pci[:, 0:1], T.pi[:, 0:1], 4, None, Op.arith_shift_right))
     done("v", V.tensor_scalar(T.pci[:, 1:2], T.pi[:, 0:1], 15, None, Op.bitwise_and))
@@ -157,54 +199,69 @@ def rank_program(g, core, T, topo):
     done("v", V.tensor_scalar(T.sl8[:, 0:8], T.fi[:, 0:8], P16, None, Op.is_equal))
     v_l8 = done("v", V.tensor_scalar(T.sl8[:, 8:16], T.fi[:, 0:8], P16, None, Op.is_gt))
 
-    need("s", v_zm)
-    SC.dma_start(T.cland[rank, 64:128, :], T.zmsg[0:16, :]).then_inc(T.sem["zd"], 16)
+    if isr:
+        need("s", v_zm)
+        SC.dma_start(T.cland[rank, 64:128, :], T.zmsg[0:16, :]).then_inc(T.sem["zd"], 16)
 
     need("v", KD, v_kc)
     for m in range(4):
         v_eq = done("v", V.tensor_scalar(T.eq[:, 64 * m:64 * m + 64], T.keyr[:], T.kk[:, 8 + m:9 + m], None, Op.is_equal))
     need("v", v_eq)
     v_ac = done("v", V.tensor_tensor_scan(T.acc[:, 1:261], T.onesb[:, 0:260], T.eq[:, 0:260], 0.0, Op.mult, Op.add))
-    need("t", v_ac, v_l8)
-    PE.matmul(T.ps0[0:8, 0:5], T.sl8[:, 8:16], T.acc[:, 256:261], True, False)
-    t_ms = done("t", PE.matmul(T.ps0[0:8, 0:5], T.sl8[:, 0:8], T.acc[:, 0:257:64], False, True))
-    need("v", t_ms)
-    v_ms = done("v", V.tensor_copy(T.msg[0:8, 0:5], T.ps0[0:8, 0:5]))
-    need("y", v_ms)
-    SY.dma_start(T.cland[rank, 0:32, :], T.msg[0:8, 0:4]).then_inc(T.sem["md"], 16)
-    need("s", v_ms)
-    SC.dma_start(T.cland[rank, 32:64, :], T.msg[0:8, 1:5]).then_inc(T.sem["md"], 16)
+    if isr:
+        need("t", v_ac, v_l8)
+        PE.matmul(T.ps0[0:8, 0:5], T.sl8[:, 8:16], T.acc[:, 256:261], True, False)
+        t_ms = done("t", PE.matmul(T.ps0[0:8, 0:5], T.sl8[:, 0:8], T.acc[:, 0:257:64], False, True))
+        need("v", t_ms)
+        v_ms = done("v", V.tensor_copy(T.msg[0:8, 0:5], T.ps0[0:8, 0:5]))
+        need("y", v_ms)
+        SY.dma_start(T.cland[rank, 0:32, :], T.msg[0:8, 0:4]).then_inc(T.sem["md"], 16)
+        need("s", v_ms)
+        SC.dma_start(T.cland[rank, 32:64, :], T.msg[0:8, 1:5]).then_inc(T.sem["md"], 16)
     MD, ZD = ("md", 32), ("zd", 16)
 
     def chain(tile, start, steps):
         tok, src = start, T.z48
-        for op, fill, base, cm, sr, st in steps:
+        for op, fill, base_, cm, sr, st in steps:
             need("p", tok)
-            tok = done("p", g.affine_select(tile[0:N, :], src[0:N, :], [[4 * sr, 4], [st, 3], [sr, 4]], op, fill, base, cm))
+            tok = done("p", g.affine_select(tile[0:N, :], src[0:N, :], [[4 * sr, 4], [st, 3], [sr, 4]], op, fill, base_, cm))
             src = tile
         return tok
-    K = 1000
-    g_wb = chain(T.wb, v_z48, [(Op.is_gt, 1.0, 0, -1, 1, K),
-                               (Op.not_equal, -1.0, -K, 1, -1, K),
-                               (Op.not_equal, 1.0, -2 * K, 1, -1, K),
-                               (Op.not_equal, -1.0, 15 + 2 * K, -1, 100, -K)])
-    g_wi = chain(T.wi, v_z48, [(Op.is_ge, 1.0, 0, 1, -1, K),
-                               (Op.not_equal, 1.0, -K, 1, -1, K),
-                               (Op.not_equal, -1.0, 1 - 2 * K, 1, -1, K)])
 
-    own = T.cland[rank]
-    need("p", MD, ZD)
-    send([([rpeer], off[0:1], "rcv", own, own),
-          ([c for c in cabp + rackp if c != rpeer], off[1:2], "cnt", own, own)])
-    spread = (off[2:] + rest)[:12]
-    send([(chipmates[j:j + 1], spread[4 * j:4 * j + 4], "cnt", own, own) for j in range(3)])
+    def weights():
+        K = 1000
+        b = chain(T.wb, v_z48, [(Op.is_gt, 1.0, 0, -1, 1, K),
+                                (Op.not_equal, -1.0, -K, 1, -1, K),
+                                (Op.not_equal, 1.0, -2 * K, 1, -1, K),
+                                (Op.not_equal, -1.0, 15 + 2 * K, -1, 100, -K)])
+        return b, chain(T.wi, v_z48, [(Op.is_ge, 1.0, 0, 1, -1, K),
+                                      (Op.not_equal, 1.0, -K, 1, -1, K),
+                                      (Op.not_equal, -1.0, 1 - 2 * K, 1, -1, K)])
+
+    own, peer = T.cland[rank], T.cland[rk(rpeer)]
     RCV = ("rcv", 1)
-    need("p", RCV)
-    peer = T.cland[rk(rpeer)]
-    send([(cabp, off[0:1], "cnt", peer, peer)])
-    CNT = ("cnt", 3 * 4 + 7 + 4)
-
-    need("y", MD, RCV, CNT)
+    if isr:
+        CNT = ("cnt", 3 + 7 + 4)
+        need("p", MD, ZD)
+        send([([rpeer], off[0:1], "rcv", own, own),
+              (cabp, off[1:2], "cnt", own, own),
+              ([c for c in rackp if c != rpeer], off[2:3], "cnt", own, own)])
+        need("p", XD)
+        send([([HELPER[core]], rest, "xd", T.xs[:], T.xs[:])])
+        send([(hof(cabp), off[3:4], "cnt", own, own),
+              (hof(rackp), off[4:5], "cnt", own, own),
+              (chipmates, rest[0:1], "cnt", own, own),
+              ([HELPER[core]], rest[1:2], "rcv", own, own)])
+        need("p", RCV)
+        send([(cabp, off[0:1], "cnt", peer, peer), (hof(cabp), off[1:2], "cnt", peer, peer)])
+        g_wb, g_wi = weights()
+        need("y", MD)
+    else:
+        CNT = ("cnt", N - 1)
+        g_wb, g_wi = weights()
+        need("p", RCV)
+        send([(hof(chipmates), rest[0:1], "cnt", own, own)])
+    need("y", RCV, CNT)
     SY.dma_start(T.cb[0:N, :], T.cland[:, 0:64, :]).then_inc(T.sem["cd"], 16)
     CD = ("cd", 16)
 
@@ -242,22 +299,19 @@ def rank_program(g, core, T, topo):
     HIF, LOF, DD = 0, 4, 8
     U4, V4, BD, JC, O4 = (T.tf[:, j:j + 4] for j in (12, 16, 20, 24, 28))
     BLK, NBLK, BLKS, BLK3 = (T.bk[:, 128 * j:128 * j + 128] for j in range(4))
-    g_cf = done("p", g.iota(T.cf[:], [[1, 64]], 0, 0, allow_small_or_imprecise_dtypes=True))
-    g_cq = done("p", g.iota(T.cq[:], [[16, 64]], TC * rank + CAP * (N - 1), 0, allow_small_or_imprecise_dtypes=True))
-    v_o4 = done("v", V.memset(O4, float(CAP)))
-    need("p", v_o4)
-    g_jc = done("p", g.affine_select(JC, O4, [[1000, 4]], Op.is_gt, float(-CAP * (N - 1)), -31, 1))
-    v_of = done("v", V.memset(T.onef[:], 1.0))
-    v_zz = done("v", V.memset(T.zz[:], 0.0))
-    v_qf = done("v", V.tensor_copy(T.qf[:], F15))
-    need("v", done("v", V.tensor_scalar(F32, T.fi[:], 5, None, Op.arith_shift_right)))
-    done("v", V.tensor_scalar(BLK, F32, P32, None, Op.is_equal))
-    done("v", V.tensor_scalar(NBLK, F32, P32, -1.0, Op.is_equal, Op.mult))
-    done("v", V.tensor_scalar(BLKS, F32, P32n, None, Op.is_equal))
-    need("v", v_of, done("v", V.tensor_scalar(T.kk[:, 5:6], P32, 3.0, -1.0, Op.is_equal, Op.mult)))
-    v_b3 = done("v", V.tensor_scalar(BLK3, T.onef[:], T.kk[:, 5:6], None, Op.mult))
-    need("v", g_cq)
-    v_ci = done("v", V.tensor_scalar(T.ci[:], T.cq[:], P15, None, Op.add))
+    if isr:
+        v_o4 = done("v", V.memset(O4, float(CAP)))
+        v_of = done("v", V.memset(T.onef[:], 1.0))
+        v_zz = done("v", V.memset(T.zz[:], 0.0))
+        v_qf = done("v", V.tensor_copy(T.qf[:], F15))
+        need("v", done("v", V.tensor_scalar(F32, T.fi[:], 5, None, Op.arith_shift_right)))
+        done("v", V.tensor_scalar(BLK, F32, P32, None, Op.is_equal))
+        done("v", V.tensor_scalar(NBLK, F32, P32, -1.0, Op.is_equal, Op.mult))
+        done("v", V.tensor_scalar(BLKS, F32, P32n, None, Op.is_equal))
+        need("v", v_of, done("v", V.tensor_scalar(T.kk[:, 5:6], P32, 3.0, -1.0, Op.is_equal, Op.mult)))
+        v_b3 = done("v", V.tensor_scalar(BLK3, T.onef[:], T.kk[:, 5:6], None, Op.mult))
+        need("v", g_cq)
+        v_ci = done("v", V.tensor_scalar(T.ci[:], T.cq[:], P15, None, Op.add))
 
     q0, m0 = rank // 4, rank % 4
     need("t", CD, g_wb, g_wi)
@@ -272,43 +326,32 @@ def rank_program(g, core, T, topo):
     need("v", t_l)
     v_o2 = done("v", V.tensor_copy(T.off2[:], T.ps5[:, 0:128]))
 
-    def gather(buf, lo, hi):
-        return done("v", V.tensor_copy(buf[:, CAP * lo:CAP * hi], T.xp[:].indirect(T.off2[:, 8 * lo:8 * hi])))
+    def gather(qn, buf, lo, n=1):
+        o, i = buf[:, CAP * lo:CAP * (lo + n)], T.xp[:].indirect(T.off2[:, 8 * lo:8 * (lo + n)])
+        need(qn, v_o2, v_xp, v_xz)
+        return done(qn, V.tensor_copy(o, i) if qn == "v" else SC.activation(o, i, Fn.Copy))
 
-    def cols(r, n=1):
-        return slice(CAP * r, CAP * (r + n))
-
-    need("v", v_o2, v_xp, v_xz)
-    dr = rk(diag[0])
-    tok = gather(T.snd, dr, dr + 4)
-    need("p", tok)
-    send([([rpeer], off[0::2], "rb", T.snd[:, cols(dr + 2, 2)], T.relb[:]),
-          ([cpeer], off[1::2], "ra", T.snd[:, cols(dr, 2)], T.rela[:])])
-    for grp in (rackp, cabp):
-        tok = gather(T.snd, rk(grp[0]), rk(grp[0]) + 4)
-    first = rank - lane
-    if lane:
-        tok = gather(T.snd, first, rank)
-    if lane < 3:
-        tok = gather(T.snd, rank + 1, first + 4)
-    v_own = gather(T.land, rank, rank + 1)
-    need("p", tok)
     mine = T.land[:, cols(rank)]
-    items = []
-    for j in range(4):
-        items.append(([rackp[j]], off[2 * j:2 * j + 1], "dat", T.snd[:, cols(rk(rackp[j]))], mine))
-        items.append(([cabp[j]], off[2 * j + 1:2 * j + 2], "dat", T.snd[:, cols(rk(cabp[j]))], mine))
-    for j in range(3):
-        items.append(([chipmates[j]], rest[2 * j:2 * j + 2], "dat", T.snd[:, cols(rk(chipmates[j]))], mine))
-    send(items)
-    need("p", ("rb", 4), ("ra", 4))
-    items = []
-    for j in range(2):
-        items.append(([rackp[j]], off[4 * j:4 * j + 4:2], "dat", T.rela[:, cols(j)], T.land[:, cols(rk(cpeer))]))
-        items.append(([cabp[2 + j]], off[4 * j + 1:4 * j + 4:2], "dat", T.relb[:, cols(j)], T.land[:, cols(rk(rpeer))]))
-    send(items)
-    DAT = ("dat", 8 + 3 * 2 + 4 * 2)
+    if isr:
+        dr = rk(diag[0])
+        need("p", gather("v", T.snd, dr, 2), gather("s", T.snd, dr + 2, 2))
+        send([([RELAY[rpeer][j]], off[2 * j:2 * j + 1], "ra", T.snd[:, cols(dr + j)], T.rela[:]) for j in range(4)])
+        need("p", gather("v", T.snd, rk(cabp[0]), 2), gather("s", T.snd, rk(cabp[2]), 2))
+        send([([cabp[j]], off[2 * j + 1:2 * j + 2], "dat", T.snd[:, cols(rk(cabp[j]))], mine) for j in range(4)])
+    else:
+        need("p", gather("v", T.snd, rk(rackp[0]), 2), gather("s", T.snd, rk(rackp[2]), 2))
+        send([([rackp[j]], off[2 * j:2 * j + 2], "dat", T.snd[:, cols(rk(rackp[j]))], mine) for j in range(4)])
+        for j in range(3):
+            need("p", gather("vsv"[j], T.snd, rk(chipmates[j])))
+        send([([chipmates[j]], rest[2 * j:2 * j + 2], "dat", T.snd[:, cols(rk(chipmates[j]))], mine) for j in range(3)])
+        need("p", ("ls", left[0]))
+        need("y", KD, XD, CD, *[(q, made[q]) for q in made])
+        return
+    v_own = gather("v", T.land, rank)
+    DAT = ("dat", 3 * 2 + 4 * 2 + 4 + 4 * len(off))
 
+    need("p", v_o4)
+    g_jc = done("p", g.affine_select(JC, O4, [[1000, 4]], Op.is_gt, float(-CAP * (N - 1)), -31, 1))
     for q in range(4):
         o, w = T.ps6[32 * q:32 * q + 32, 0:12], slice(12 * q, 12 * q + 12)
         PE.matmul(o, T.cb[0:N, 0:32], T.wb[0:N, w], True, False)
@@ -345,13 +388,16 @@ def rank_program(g, core, T, topo):
     need("v", done("v", V.tensor_tensor(T.w1[:], T.ps1[:, 0:64], T.ci[:], Op.add)), t_15)
     v_o3 = done("v", V.tensor_scalar(T.off3[:], T.w1[:], T.ps2[:, 0:1], None, Op.add))
 
-    need("v", v_o3, v_own, DAT)
-    for j in range(4):
+    tok = {}
+    for j in (0, 2, 1, 3):
+        w, i = slice(256 * j, 256 * j + 256), T.land[:].indirect(T.off3[:, 16 * j:16 * j + 16])
+        qn = "v" if j < 2 else "s"
+        need(qn, v_o3, v_own, DAT)
+        tok[j] = done(qn, V.tensor_copy(T.yb[:, w], i) if j < 2 else SC.activation(T.yb[:, w], i, Fn.Copy))
+    for j, qn in ((0, "y"), (2, "y"), (1, "y"), (3, "s")):
         w = slice(256 * j, 256 * j + 256)
-        tok = done("v", V.tensor_copy(T.yb[:, w], T.land[:].indirect(T.off3[:, 16 * j:16 * j + 16])))
-        qn = "ys"[j % 2]
-        need(qn, tok)
+        need(qn, tok[j])
         queue[qn].dma_start(T.y[:, w], T.yb[:, w]).then_inc(T.sem["yd"], 16)
 
     need("p", ("ls", left[0]))
-    need("y", ("v", made["v"]), ("t", made["t"]), ("p", made["p"]), KD, XD, MD, ZD, CD, ("yd", 64))
+    need("y", KD, XD, MD, ZD, CD, ("yd", 64), *[(q, made[q]) for q in made])

@@ -36,9 +36,7 @@ SCRATCH = {
     "selb": ("sbuf", [128, 128], "bfloat16"),
     "lc": ("sbuf", [128, 128], "bfloat16"),
     "d8": ("sbuf", [128, 128], "float32"),
-    "z48": ("sbuf", [128, 48], "float32"),
-    "wb": ("sbuf", [128, 48], "float32"),
-    "wi": ("sbuf", [128, 48], "float32"),
+    "wt": ("sbuf", [128, 96], "float32"),
     "cb": ("sbuf", [128, 64], "float32"),
     "c1": ("sbuf", [128, 128], "float32"),
     "c2": ("sbuf", [128, 128], "bfloat16"),
@@ -62,7 +60,8 @@ for _k in range(8):
     SCRATCH["ps%d" % _k] = ("psum", [128, 512], "float32")
 
 SEMAPHORES = ["v", "t", "p", "s",
-              "kd", "xd",
+              "kd", "xd", "xe",
+              "wd",
               "md", "zd", "cd", "yd",
               "cnt", "rcv", "ra", "rb", "dat",
               "ls"]
@@ -130,9 +129,6 @@ def rank_program(g, core, T, topo):
             e += 1
         return out
 
-    off = [e for e in engines(rpeer) if e in engines(cpeer)]
-    rest = [e for e in engines(chipmates[0]) if e not in off]
-
     def mask(es):
         return sum(1 << e for e in es)
 
@@ -153,20 +149,32 @@ def rank_program(g, core, T, topo):
     def cols(r, n=1):
         return slice(CAP * r, CAP * (r + n))
 
+    off = engines(rpeer)
+    even, odd = off[0::2], off[1::2]
+    MINE, HIS = (0, 1), (2, 3)
+    first = {j: even[2 * j:2 * j + 2] for j in MINE}
+    first.update({j: off[4 * (j - 2):4 * (j - 2) + 4] for j in HIS})
+
     if core in RELAY[base]:
         j = RELAY[base].index(core)
-        need("p", ("ra", 1))
+        need("p", ("ra", len(first[j])))
         send([([RELAY[cpeer][j]], off, "rb", T.rela[:], T.relb[:])])
         need("p", ("rb", len(off)))
         send([([chip4[j]], off, "dat", T.relb[:], T.land[:, cols(rk(diag[lane]))])])
         need("p", ("ls", left[0]))
         return
 
+    rest = [e for e in engines(chipmates[0]) if e not in off]
+
+    H, Q = TC // 2, 3 * TC // 4
     if isr:
         for j in range(8):
             (SY if j % 2 == 0 else SC).dma_start(T.keyr[16 * j:16 * j + 16, :], T.key[:]).then_inc(T.sem["kd"], 16)
-        SC.dma_start(T.xs[:], T.x[:]).then_inc(T.sem["xd"], 16)
-    KD, XD = (("kd", 128), ("xd", 16)) if isr else (("kd", len(off)), ("xd", len(rest)))
+        SC.dma_start(T.xs[:, 0:H], T.x[:, 0:H]).then_inc(T.sem["xd"], 16)
+        SY.dma_start(T.xs[:, H:], T.x[:, H:]).then_inc(T.sem["xe"], 16)
+        KD, XD, XE = ("kd", 128), ("xd", 16), ("xe", 16)
+    else:
+        KD, XD, XE = ("kd", 4), ("xd", len(rest)), ("xe", len(rest) + 4)
 
     g_pi = done("p", g.iota(T.pi[:], [[32, 2]], 0, 1))
     g_m4 = done("p", g.iota(T.kk[:, 0:4], [[1, 4]], 0, 0, allow_small_or_imprecise_dtypes=True))
@@ -174,17 +182,18 @@ def rank_program(g, core, T, topo):
     g_lc = done("p", g.iota(T.lc[0:16, :], [[0, 16], [16, 8]], 0, 1, allow_small_or_imprecise_dtypes=True))
     g_d8 = done("p", g.iota(T.d8[0:32, :], [[TC, 16], [0, 8]], 0, 0, allow_small_or_imprecise_dtypes=True))
     if isr:
-        g_cf = done("p", g.iota(T.cf[:], [[1, 64]], 0, 0, allow_small_or_imprecise_dtypes=True))
-        g_cq = done("p", g.iota(T.cq[:], [[16, 64]], TC * rank + CAP * (N - 1), 0, allow_small_or_imprecise_dtypes=True))
         need("p", KD)
-        send([([HELPER[core]], off, "kd", T.keyr[:], T.keyr[:])])
+        send([([HELPER[core]], off[0:4], "kd", T.keyr[:], T.keyr[:])])
+        need("p", XD)
+        send([([HELPER[core]], rest, "xd", T.xs[:, 0:H], T.xs[:, 0:H])])
 
     done("v", V.memset(T.onesb[:], 1.0))
     done("v", V.memset(T.eq[:, 256:264], 0.0))
     done("v", V.memset(T.acc[:, 0:1], 0.0))
-    v_z48 = done("v", V.memset(T.z48[:], 0.0))
     if isr:
         v_zm = done("v", V.memset(T.zmsg[:], 0.0))
+    else:
+        v_wt = done("v", V.memset(T.wt[:], 0.0))
     need("v", g_pi, g_m4)
     done("v", V.tensor_scalar(T.pci[:, 0:1], T.pi[:, 0:1], 4, None, Op.arith_shift_right))
     done("v", V.tensor_scalar(T.pci[:, 1:2], T.pi[:, 0:1], 15, None, Op.bitwise_and))
@@ -220,48 +229,48 @@ def rank_program(g, core, T, topo):
         SC.dma_start(T.cland[rank, 32:64, :], T.msg[0:8, 1:5]).then_inc(T.sem["md"], 16)
     MD, ZD = ("md", 32), ("zd", 16)
 
-    def chain(tile, start, steps):
-        tok, src = start, T.z48
+    WB, WI = T.wt[0:N, 0:48], T.wt[0:N, 48:96]
+
+    def chain(tile, tok, steps):
         for op, fill, base_, cm, sr, st in steps:
             need("p", tok)
-            tok = done("p", g.affine_select(tile[0:N, :], src[0:N, :], [[4 * sr, 4], [st, 3], [sr, 4]], op, fill, base_, cm))
-            src = tile
+            tok = done("p", g.affine_select(tile, tile, [[4 * sr, 4], [st, 3], [sr, 4]], op, fill, base_, cm))
         return tok
 
     def weights():
         K = 1000
-        b = chain(T.wb, v_z48, [(Op.is_gt, 1.0, 0, -1, 1, K),
-                                (Op.not_equal, -1.0, -K, 1, -1, K),
-                                (Op.not_equal, 1.0, -2 * K, 1, -1, K),
-                                (Op.not_equal, -1.0, 15 + 2 * K, -1, 100, -K)])
-        return b, chain(T.wi, v_z48, [(Op.is_ge, 1.0, 0, 1, -1, K),
-                                      (Op.not_equal, 1.0, -K, 1, -1, K),
-                                      (Op.not_equal, -1.0, 1 - 2 * K, 1, -1, K)])
+        b = chain(WB, v_wt, [(Op.is_gt, 1.0, 0, -1, 1, K),
+                             (Op.not_equal, -1.0, -K, 1, -1, K),
+                             (Op.not_equal, 1.0, -2 * K, 1, -1, K),
+                             (Op.not_equal, -1.0, 15 + 2 * K, -1, 100, -K)])
+        return b, chain(WI, v_wt, [(Op.is_ge, 1.0, 0, 1, -1, K),
+                                   (Op.not_equal, 1.0, -K, 1, -1, K),
+                                   (Op.not_equal, -1.0, 1 - 2 * K, 1, -1, K)])
 
     own, peer = T.cland[rank], T.cland[rk(rpeer)]
-    RCV = ("rcv", 1)
     if isr:
-        CNT = ("cnt", 3 + 7 + 4)
+        RCV, CNT, WD = [("rcv", 1)], ("cnt", 3 + 3 + 4 + 4), [("wd", len(off))]
         need("p", MD, ZD)
         send([([rpeer], off[0:1], "rcv", own, own),
               (cabp, off[1:2], "cnt", own, own),
               ([c for c in rackp if c != rpeer], off[2:3], "cnt", own, own)])
-        need("p", XD)
-        send([([HELPER[core]], rest, "xd", T.xs[:], T.xs[:])])
-        send([(hof(cabp), off[3:4], "cnt", own, own),
-              (hof(rackp), off[4:5], "cnt", own, own),
-              (chipmates, rest[0:1], "cnt", own, own),
-              ([HELPER[core]], rest[1:2], "rcv", own, own)])
-        need("p", RCV)
+        send([(hof(cabp), off[0:1], "cnt", own, own),
+              (hof(rackp), off[1:2], "cnt", own, own),
+              (chipmates, off[2:3], "cnt", own, own),
+              (hof(chip4), off[3:4], "cnt", own, own)])
+        need("p", XE)
+        send([([HELPER[core]], rest, "xe", T.xs[:, H:Q], T.xs[:, H:Q]),
+              ([HELPER[core]], off[4:8], "xe", T.xs[:, Q:], T.xs[:, Q:])])
+        need("p", *RCV)
         send([(cabp, off[0:1], "cnt", peer, peer), (hof(cabp), off[1:2], "cnt", peer, peer)])
-        g_wb, g_wi = weights()
-        need("y", MD)
+        g_cf = done("p", g.iota(T.cf[:], [[1, 64]], 0, 0, allow_small_or_imprecise_dtypes=True))
+        g_cq = done("p", g.iota(T.cq[:], [[16, 64]], TC * rank + CAP * (N - 1), 0, allow_small_or_imprecise_dtypes=True))
+        need("y", MD, ZD)
     else:
-        CNT = ("cnt", N - 1)
-        g_wb, g_wi = weights()
-        need("p", RCV)
-        send([(hof(chipmates), rest[0:1], "cnt", own, own)])
-    need("y", RCV, CNT)
+        RCV, CNT, WD = [], ("cnt", N), list(weights())
+        need("p", *WD)
+        send([([base], off, "wd", T.wt[:], T.wt[:])])
+    need("y", CNT, *RCV)
     SY.dma_start(T.cb[0:N, :], T.cland[:, 0:64, :]).then_inc(T.sem["cd"], 16)
     CD = ("cd", 16)
 
@@ -277,7 +286,7 @@ def rank_program(g, core, T, topo):
     v_sb = done("v", V.tensor_scalar(T.selb[:], F15, P15, None, Op.is_equal))
     need("v", v_ws, v_wle)
     v_wn = done("v", V.tensor_tensor(T.wneg[:], T.wle[:], T.wsame[:], Op.mult))
-    need("t", v_wl)
+    need("t", v_ac, v_wl)
     t_b = done("t", PE.matmul(T.ps2[:, 0:1], T.wlt[:], T.acc[:, 256:257], True, True))
     need("t", v_wn)
     PE.matmul(T.ps1[:, 0:256], T.wsame[:], T.acc[:, 1:257], True, False)
@@ -293,30 +302,19 @@ def rank_program(g, core, T, topo):
     t_p = done("t", ins)
     v_xz = done("v", V.memset(T.xp[:, TC:], 0.0))
     need("v", t_p)
-    need("v", done("v", V.tensor_copy(T.off1[:], T.ps3[:, 0:64])), XD)
-    v_xp = done("v", V.tensor_copy(T.xp[:, 0:TC].indirect(T.off1[:]), T.xs[:]))
+    need("v", done("v", V.tensor_copy(T.off1[:], T.ps3[:, 0:64])))
 
-    HIF, LOF, DD = 0, 4, 8
-    U4, V4, BD, JC, O4 = (T.tf[:, j:j + 4] for j in (12, 16, 20, 24, 28))
-    BLK, NBLK, BLKS, BLK3 = (T.bk[:, 128 * j:128 * j + 128] for j in range(4))
-    if isr:
-        v_o4 = done("v", V.memset(O4, float(CAP)))
-        v_of = done("v", V.memset(T.onef[:], 1.0))
-        v_zz = done("v", V.memset(T.zz[:], 0.0))
-        v_qf = done("v", V.tensor_copy(T.qf[:], F15))
-        need("v", done("v", V.tensor_scalar(F32, T.fi[:], 5, None, Op.arith_shift_right)))
-        done("v", V.tensor_scalar(BLK, F32, P32, None, Op.is_equal))
-        done("v", V.tensor_scalar(NBLK, F32, P32, -1.0, Op.is_equal, Op.mult))
-        done("v", V.tensor_scalar(BLKS, F32, P32n, None, Op.is_equal))
-        need("v", v_of, done("v", V.tensor_scalar(T.kk[:, 5:6], P32, 3.0, -1.0, Op.is_equal, Op.mult)))
-        v_b3 = done("v", V.tensor_scalar(BLK3, T.onef[:], T.kk[:, 5:6], None, Op.mult))
-        need("v", g_cq)
-        v_ci = done("v", V.tensor_scalar(T.ci[:], T.cq[:], P15, None, Op.add))
+    def scatter(a, b, *toks):
+        need("v", *toks)
+        return done("v", V.tensor_copy(T.xp[:, 0:TC].indirect(T.off1[:, 8 * a:8 * b]), T.xs[:, cols(a, b - a)]))
+
+    v_xp = scatter(0, 8, XD, XE) if isr else scatter(4, 8, scatter(0, 4, XD), XE)
 
     q0, m0 = rank // 4, rank % 4
-    need("t", CD, g_wb, g_wi)
-    PE.matmul(T.ps4[0:32, 0:12], T.cb[0:N, 0:32], T.wb[0:N, 12 * q0:12 * q0 + 12], True, False)
-    t_s = done("t", PE.matmul(T.ps4[0:32, 0:12], T.cb[0:N, 32:64], T.wi[0:N, 12 * q0:12 * q0 + 12], False, True))
+    wq = lambda q: (T.wt[0:N, 12 * q:12 * q + 12], T.wt[0:N, 48 + 12 * q:60 + 12 * q])
+    need("t", CD, *WD)
+    PE.matmul(T.ps4[0:32, 0:12], T.cb[0:N, 0:32], wq(q0)[0], True, False)
+    t_s = done("t", PE.matmul(T.ps4[0:32, 0:12], T.cb[0:N, 32:64], wq(q0)[1], False, True))
     need("v", t_s, g_d8)
     v_c1 = done("v", V.tensor_scalar(T.c1[0:32, :], T.d8[0:32, :], T.ps4[0:32, m0:m0 + 1], 0.0, Op.subtract, Op.max))
     need("v", v_c1)
@@ -331,31 +329,49 @@ def rank_program(g, core, T, topo):
         need(qn, v_o2, v_xp, v_xz)
         return done(qn, V.tensor_copy(o, i) if qn == "v" else SC.activation(o, i, Fn.Copy))
 
-    mine = T.land[:, cols(rank)]
-    if isr:
-        dr = rk(diag[0])
-        need("p", gather("v", T.snd, dr, 2), gather("s", T.snd, dr + 2, 2))
-        send([([RELAY[rpeer][j]], off[2 * j:2 * j + 1], "ra", T.snd[:, cols(dr + j)], T.rela[:]) for j in range(4)])
-        need("p", gather("v", T.snd, rk(cabp[0]), 2), gather("s", T.snd, rk(cabp[2]), 2))
-        send([([cabp[j]], off[2 * j + 1:2 * j + 2], "dat", T.snd[:, cols(rk(cabp[j]))], mine) for j in range(4)])
-    else:
-        need("p", gather("v", T.snd, rk(rackp[0]), 2), gather("s", T.snd, rk(rackp[2]), 2))
-        send([([rackp[j]], off[2 * j:2 * j + 2], "dat", T.snd[:, cols(rk(rackp[j]))], mine) for j in range(4)])
-        for j in range(3):
-            need("p", gather("vsv"[j], T.snd, rk(chipmates[j])))
-        send([([chipmates[j]], rest[2 * j:2 * j + 2], "dat", T.snd[:, cols(rk(chipmates[j]))], mine) for j in range(3)])
+    mine, snd = T.land[:, cols(rank)], lambda c: T.snd[:, cols(rk(c))]
+    a, b = MINE if isr else HIS
+    near = chipmates[0:1] if isr else chipmates[1:]
+
+    def two(cs):
+        return [gather("v", T.snd, rk(cs[a])), gather("s", T.snd, rk(cs[b]))]
+
+    need("p", *two(diag))
+    send([([RELAY[rpeer][j]], first[j], "ra", snd(diag[j]), T.rela[:]) for j in (a, b)])
+    need("p", *two(cabp))
+    send([([cabp[j]], odd[2 * i:2 * i + 2], "dat", snd(cabp[j]), mine) for i, j in enumerate((a, b))])
+    need("p", *two(rackp), *[gather("sv"[j], T.snd, rk(c)) for j, c in enumerate(near)])
+    send([([rackp[j]], even[2 * i:2 * i + 2], "dat", snd(rackp[j]), mine) for i, j in enumerate((a, b))]
+         + [([c], rest[2 * j:2 * j + 2], "dat", snd(c), mine) for j, c in enumerate(near)])
+    if not isr:
         need("p", ("ls", left[0]))
-        need("y", KD, XD, CD, *[(q, made[q]) for q in made])
+        need("y", KD, XD, XE, CD, *[(q, made[q]) for q in made])
         return
     v_own = gather("v", T.land, rank)
-    DAT = ("dat", 3 * 2 + 4 * 2 + 4 + 4 * len(off))
+    DAT = ("dat", 2 * (3 + 4 + 4) + 4 * len(off))
+
+    HIF, LOF, DD = 0, 4, 8
+    U4, V4, BD, JC, O4 = (T.tf[:, j:j + 4] for j in (12, 16, 20, 24, 28))
+    BLK, NBLK, BLKS, BLK3 = (T.bk[:, 128 * j:128 * j + 128] for j in range(4))
+    v_o4 = done("v", V.memset(O4, float(CAP)))
+    v_of = done("v", V.memset(T.onef[:], 1.0))
+    v_zz = done("v", V.memset(T.zz[:], 0.0))
+    v_qf = done("v", V.tensor_copy(T.qf[:], F15))
+    need("v", done("v", V.tensor_scalar(F32, T.fi[:], 5, None, Op.arith_shift_right)))
+    done("v", V.tensor_scalar(BLK, F32, P32, None, Op.is_equal))
+    done("v", V.tensor_scalar(NBLK, F32, P32, -1.0, Op.is_equal, Op.mult))
+    done("v", V.tensor_scalar(BLKS, F32, P32n, None, Op.is_equal))
+    need("v", v_of, done("v", V.tensor_scalar(T.kk[:, 5:6], P32, 3.0, -1.0, Op.is_equal, Op.mult)))
+    v_b3 = done("v", V.tensor_scalar(BLK3, T.onef[:], T.kk[:, 5:6], None, Op.mult))
+    need("v", g_cq)
+    v_ci = done("v", V.tensor_scalar(T.ci[:], T.cq[:], P15, None, Op.add))
 
     need("p", v_o4)
     g_jc = done("p", g.affine_select(JC, O4, [[1000, 4]], Op.is_gt, float(-CAP * (N - 1)), -31, 1))
     for q in range(4):
-        o, w = T.ps6[32 * q:32 * q + 32, 0:12], slice(12 * q, 12 * q + 12)
-        PE.matmul(o, T.cb[0:N, 0:32], T.wb[0:N, w], True, False)
-        t_y = done("t", PE.matmul(o, T.cb[0:N, 32:64], T.wi[0:N, w], False, True))
+        o = T.ps6[32 * q:32 * q + 32, 0:12]
+        PE.matmul(o, T.cb[0:N, 0:32], wq(q)[0], True, False)
+        t_y = done("t", PE.matmul(o, T.cb[0:N, 32:64], wq(q)[1], False, True))
     need("v", t_y, g_jc)
     v_ti = done("v", V.tensor_scalar(T.ti[:, 0:4], T.ps6[:, 0:4], float(TC * rank), None, Op.subtract))
     v_u = done("v", V.tensor_scalar(U4, T.ps6[:, 0:4], -1.0, float(TC * rank), Op.mult, Op.add))
@@ -376,7 +392,7 @@ def rank_program(g, core, T, topo):
     v_dd = done("v", V.tensor_tensor(T.tf[:, DD:DD + 4], T.ps7[:, 0:4], BD, Op.add))
     need("v", v_dd, v_qf, g_cf)
     for m in range(4):
-        hi, lo, jump = (T.tf[:, b + m:b + m + 1] for b in (HIF, LOF, DD))
+        hi, lo, jump = (T.tf[:, b_ + m:b_ + m + 1] for b_ in (HIF, LOF, DD))
         lm, r1, r2 = T.lm[:, 128 * m:128 * m + 128], T.r1[:, 64 * m:64 * m + 64], T.r2[:, 64 * m:64 * m + 64]
         done("v", V.tensor_scalar(lm, T.qf[:], lo, None, Op.is_ge))
         done("v", V.tensor_scalar(r1, T.cf[:], hi, jump, Op.is_equal, Op.mult))
@@ -400,4 +416,4 @@ def rank_program(g, core, T, topo):
         queue[qn].dma_start(T.y[:, w], T.yb[:, w]).then_inc(T.sem["yd"], 16)
 
     need("p", ("ls", left[0]))
-    need("y", KD, XD, MD, ZD, CD, ("yd", 64), *[(q, made[q]) for q in made])
+    need("y", KD, XD, XE, MD, ZD, CD, *WD, ("yd", 64), *[(q, made[q]) for q in made])

from concourse.bass import DstId, RemoteDMATransfer
from concourse.mybir import AluOpType as Op, ActivationFunctionType as Fn

N, TC, CAP = 16, 1024, 128

SCRATCH = {
    "xs": ("sbuf", [128, TC], "float32"),
    "xp": ("sbuf", [128, TC + CAP], "float32"),
    "snd": ("sbuf", [128, N * CAP], "float32"),
    "land": ("sbuf", [128, N * CAP], "float32"),
    "rela": ("sbuf", [128, CAP], "float32"),
    "relb": ("sbuf", [128, CAP], "float32"),
    "yb": ("sbuf", [128, TC], "float32"),
    "cland": ("dram", [N, 128, 1], "float32"),
    "keyr": ("sbuf", [128, 64], "int32"),
    "pi": ("sbuf", [128, 2], "int32"),
    "fi": ("sbuf", [128, 128], "int32"),
    "fb": ("sbuf", [128, 384], "int32"),
    "kk": ("sbuf", [128, 16], "float32"),
    "pci": ("sbuf", [128, 8], "int32"),
    "pcf": ("sbuf", [128, 8], "float32"),
    "onesb": ("sbuf", [128, 264], "bfloat16"),
    "eq": ("sbuf", [128, 264], "bfloat16"),
    "acc": ("sbuf", [128, 264], "bfloat16"),
    "sl8": ("sbuf", [128, 16], "bfloat16"),
    "msg": ("sbuf", [128, 8], "float32"),
    "zmsg": ("sbuf", [128, 4], "float32"),
    "wsame": ("sbuf", [128, 128], "bfloat16"),
    "wle": ("sbuf", [128, 128], "bfloat16"),
    "wneg": ("sbuf", [128, 128], "bfloat16"),
    "wlt": ("sbuf", [128, 128], "bfloat16"),
    "selq": ("sbuf", [128, 128], "float32"),
    "rb": ("sbuf", [128, 256], "float32"),
    "rbe": ("sbuf", [128, 256], "float32"),
    "off1": ("sbuf", [128, 64], "uint16"),
    "selb": ("sbuf", [128, 128], "bfloat16"),
    "lc": ("sbuf", [128, 128], "bfloat16"),
    "d8": ("sbuf", [128, 128], "float32"),
    "wt": ("sbuf", [128, 96], "float32"),
    "cb": ("sbuf", [128, 64], "float32"),
    "c1": ("sbuf", [128, 128], "float32"),
    "c2": ("sbuf", [128, 128], "bfloat16"),
    "off2": ("sbuf", [128, 128], "uint16"),
    "bk": ("sbuf", [128, 512], "bfloat16"),
    "zz": ("sbuf", [128, 8], "bfloat16"),
    "ti": ("sbuf", [128, 12], "int32"),
    "tf": ("sbuf", [128, 32], "float32"),
    "qf": ("sbuf", [128, 128], "float32"),
    "cf": ("sbuf", [128, 64], "float32"),
    "cq": ("sbuf", [128, 64], "float32"),
    "ci": ("sbuf", [128, 64], "float32"),
    "onef": ("sbuf", [128, 128], "float32"),
    "lm": ("sbuf", [128, 512], "float32"),
    "r1": ("sbuf", [128, 256], "float32"),
    "r2": ("sbuf", [128, 256], "float32"),
    "w1": ("sbuf", [128, 64], "float32"),
    "off3": ("sbuf", [128, 64], "uint16"),
}
for _k in range(8):
    SCRATCH["ps%d" % _k] = ("psum", [128, 512], "float32")

SEMAPHORES = ["v", "t", "p", "s",
              "kd", "xd", "xe",
              "wd",
              "md", "zd", "cd", "yd",
              "cnt", "rcv", "ra", "rb", "dat",
              "ls"]
HELPER, RELAY = {}, {}


def plan(cores, topo):
    if HELPER:
        return
    world = range(512)
    spot = lambda k: (topo.host(k), topo.chip(k))
    for c in cores:
        side = [k for k in world if spot(k) == spot(c) and topo.die(k) == topo.die(c)]
        idle = [k for k in side if k not in cores]
        HELPER[c] = idle[[k for k in side if k in cores].index(c)]
        here = [k for k in world if spot(k) == spot(c)].index(c)
        others = sorted({topo.chip(k) for k in world if topo.host(k) == topo.host(c) and topo.same_plane(k, c)})
        RELAY[c] = [[k for k in world if spot(k) == (topo.host(c), e)][here] for e in others[:4]]


def rank_program(g, core, T, topo):
    place = lambda c: (topo.host(c), topo.chip(c))
    cores = list(T.cores)
    plan(cores, topo)
    base = None
    for c in cores:
        if core in (c, HELPER[c]) or core in RELAY[c]:
            base = c
    if base is None:
        return
    rank, isr = T.rank_of(base), core == base
    V, PE, SY, SC = g.vector, g.tensor, g.sync, g.scalar
    queue = {"v": V, "t": PE, "p": g, "y": SY, "s": SC}
    made, known = {"v": 0, "t": 0, "p": 0, "s": 0}, {}

    def need(qn, *toks):
        most = {}
        for s, n in toks:
            most[s] = max(n, most.get(s, 0))
        for s in most:
            if known.get((qn, s), 0) < most[s]:
                queue[qn].wait_ge(T.sem[s], most[s])
                known[(qn, s)] = most[s]

    def done(qn, ins):
        made[qn] += 1
        ins.then_inc(T.sem[qn], 1)
        return (qn, made[qn])

    chipmates = [c for c in cores if c != base and place(c) == place(base)]
    chip4 = sorted(chipmates + [base])
    rackp = [c for c in cores if topo.same_plane(base, c)]
    cabp = [c for c in cores if topo.may_write(base, c) and topo.rack(topo.host(c)) != topo.rack(topo.host(base))]
    diag = [c for c in cores if c != base and not topo.may_write(base, c)]
    lane = chip4.index(base)
    rpeer, cpeer = rackp[lane], cabp[lane]
    rk = T.rank_of
    hof = lambda cs: [HELPER[c] for c in cs]

    def engines(dst):
        m, e, out = topo.mask(core, dst), 0, []
        while m >> e:
            if (m >> e) & 1:
                out.append(e)
            e += 1
        return out

    def mask(es):
        return sum(1 << e for e in es)

    def dst(c):
        rid, pid = topo.addr(c, core)
        return DstId(rid=rid, pnc=pid)

    left = [0]

    def send(items):
        ts = []
        for to, es, sem, src, out in items:
            ts.append(RemoteDMATransfer(dst_ids=[dst(c) for c in to], dma_engine_mask=mask(es), remote_sem=T.sem[sem],
                                        srcs=[src], dsts=[out for c in to]))
            left[0] += len(es)
        g.remote_dma_fused(ts, local_sem=T.sem["ls"])

    def cols(r, n=1):
        return slice(CAP * r, CAP * (r + n))

    off = engines(rpeer)
    even, odd = off[0::2], off[1::2]
    MINE, HIS = (0, 1), (2, 3)
    first = {j: even[2 * j:2 * j + 2] for j in MINE}
    first.update({j: off[4 * (j - 2):4 * (j - 2) + 4] for j in HIS})

    if core in RELAY[base]:
        j = RELAY[base].index(core)
        need("p", ("ra", len(first[j])))
        send([([RELAY[cpeer][j]], off, "rb", T.rela[:], T.relb[:])])
        need("p", ("rb", len(off)))
        send([([chip4[j]], off, "dat", T.relb[:], T.land[:, cols(rk(diag[lane]))])])
        need("p", ("ls", left[0]))
        return

    rest = [e for e in engines(chipmates[0]) if e not in off]

    H, Q = TC // 2, 3 * TC // 4
    if isr:
        for j in range(8):
            (SY if j % 2 == 0 else SC).dma_start(T.keyr[16 * j:16 * j + 16, :], T.key[:]).then_inc(T.sem["kd"], 16)
        SC.dma_start(T.xs[:, 0:H], T.x[:, 0:H]).then_inc(T.sem["xd"], 16)
        SY.dma_start(T.xs[:, H:], T.x[:, H:]).then_inc(T.sem["xe"], 16)
        KD, XD, XE = ("kd", 128), ("xd", 16), ("xe", 16)
    else:
        KD, XD, XE = ("kd", 4), ("xd", len(rest)), ("xe", len(rest) + 4)

    g_pi = done("p", g.iota(T.pi[:], [[32, 2]], 0, 1))
    g_m4 = done("p", g.iota(T.kk[:, 0:4], [[1, 4]], 0, 0, allow_small_or_imprecise_dtypes=True))
    g_fi = done("p", g.iota(T.fi[:], [[1, 128]], 0, 0))
    g_lc = done("p", g.iota(T.lc[0:16, :], [[0, 16], [16, 8]], 0, 1, allow_small_or_imprecise_dtypes=True))
    g_d8 = done("p", g.iota(T.d8[0:32, :], [[TC, 16], [0, 8]], 0, 0, allow_small_or_imprecise_dtypes=True))
    if isr:
        need("p", KD)
        send([([HELPER[core]], off[0:4], "kd", T.keyr[:], T.keyr[:])])
        need("p", XD)
        send([([HELPER[core]], rest, "xd", T.xs[:, 0:H], T.xs[:, 0:H])])

    done("v", V.memset(T.onesb[:], 1.0))
    done("v", V.memset(T.eq[:, 256:264], 0.0))
    done("v", V.memset(T.acc[:, 0:1], 0.0))
    if isr:
        v_zm = done("v", V.memset(T.zmsg[:], 0.0))
    else:
        v_wt = done("v", V.memset(T.wt[:], 0.0))
    need("v", g_pi, g_m4)
    done("v", V.tensor_scalar(T.pci[:, 0:1], T.pi[:, 0:1], 4, None, Op.arith_shift_right))
    done("v", V.tensor_scalar(T.pci[:, 1:2], T.pi[:, 0:1], 15, None, Op.bitwise_and))
    done("v", V.tensor_scalar(T.pci[:, 2:3], T.pi[:, 0:1], 5, None, Op.arith_shift_right))
    done("v", V.tensor_scalar(T.pci[:, 3:4], T.pi[:, 1:2], 5, 3, Op.arith_shift_right, Op.bitwise_and))
    need("v", done("v", V.tensor_copy(T.pci[:, 4:5], T.pi[:, 0:1])))
    need("v", done("v", V.tensor_copy(T.pcf[:, 0:5], T.pci[:, 0:5])))
    P16, P15, P32, P32n, P0 = (T.pcf[:, j:j + 1] for j in range(5))
    need("v", done("v", V.tensor_scalar(T.kk[:, 4:5], P16, 4.0, None, Op.mult)))
    v_kc = done("v", V.tensor_scalar(T.kk[:, 8:12], T.kk[:, 0:4], T.kk[:, 4:5], None, Op.add))
    need("v", g_fi)
    done("v", V.tensor_scalar(T.sl8[:, 0:8], T.fi[:, 0:8], P16, None, Op.is_equal))
    v_l8 = done("v", V.tensor_scalar(T.sl8[:, 8:16], T.fi[:, 0:8], P16, None, Op.is_gt))

    if isr:
        need("s", v_zm)
        SC.dma_start(T.cland[rank, 64:128, :], T.zmsg[0:16, :]).then_inc(T.sem["zd"], 16)

    need("v", KD, v_kc)
    for m in range(4):
        v_eq = done("v", V.tensor_scalar(T.eq[:, 64 * m:64 * m + 64], T.keyr[:], T.kk[:, 8 + m:9 + m], None, Op.is_equal))
    need("v", v_eq)
    v_ac = done("v", V.tensor_tensor_scan(T.acc[:, 1:261], T.onesb[:, 0:260], T.eq[:, 0:260], 0.0, Op.mult, Op.add))
    if isr:
        need("t", v_ac, v_l8)
        PE.matmul(T.ps0[0:8, 0:5], T.sl8[:, 8:16], T.acc[:, 256:261], True, False)
        t_ms = done("t", PE.matmul(T.ps0[0:8, 0:5], T.sl8[:, 0:8], T.acc[:, 0:257:64], False, True))
        need("v", t_ms)
        v_ms = done("v", V.tensor_copy(T.msg[0:8, 0:5], T.ps0[0:8, 0:5]))
        need("y", v_ms)
        SY.dma_start(T.cland[rank, 0:32, :], T.msg[0:8, 0:4]).then_inc(T.sem["md"], 16)
        need("s", v_ms)
        SC.dma_start(T.cland[rank, 32:64, :], T.msg[0:8, 1:5]).then_inc(T.sem["md"], 16)
    MD, ZD = ("md", 32), ("zd", 16)

    WB, WI = T.wt[0:N, 0:48], T.wt[0:N, 48:96]

    def chain(tile, tok, steps):
        for op, fill, base_, cm, sr, st in steps:
            need("p", tok)
            tok = done("p", g.affine_select(tile, tile, [[4 * sr, 4], [st, 3], [sr, 4]], op, fill, base_, cm))
        return tok

    def weights():
        K = 1000
        b = chain(WB, v_wt, [(Op.is_gt, 1.0, 0, -1, 1, K),
                             (Op.not_equal, -1.0, -K, 1, -1, K),
                             (Op.not_equal, 1.0, -2 * K, 1, -1, K),
                             (Op.not_equal, -1.0, 15 + 2 * K, -1, 100, -K)])
        return b, chain(WI, v_wt, [(Op.is_ge, 1.0, 0, 1, -1, K),
                                   (Op.not_equal, 1.0, -K, 1, -1, K),
                                   (Op.not_equal, -1.0, 1 - 2 * K, 1, -1, K)])

    own, peer = T.cland[rank], T.cland[rk(rpeer)]
    if isr:
        RCV, CNT, WD = [("rcv", 1)], ("cnt", 3 + 3 + 4 + 4), [("wd", len(off))]
        need("p", MD, ZD)
        send([([rpeer], off[0:1], "rcv", own, own),
              (cabp, off[1:2], "cnt", own, own),
              ([c for c in rackp if c != rpeer], off[2:3], "cnt", own, own)])
        send([(hof(cabp), off[0:1], "cnt", own, own),
              (hof(rackp), off[1:2], "cnt", own, own),
              (chipmates, off[2:3], "cnt", own, own),
              (hof(chip4), off[3:4], "cnt", own, own)])
        need("p", XE)
        send([([HELPER[core]], rest, "xe", T.xs[:, H:Q], T.xs[:, H:Q]),
              ([HELPER[core]], off[4:8], "xe", T.xs[:, Q:], T.xs[:, Q:])])
        need("p", *RCV)
        send([(cabp, off[0:1], "cnt", peer, peer), (hof(cabp), off[1:2], "cnt", peer, peer)])
        g_cf = done("p", g.iota(T.cf[:], [[1, 64]], 0, 0, allow_small_or_imprecise_dtypes=True))
        g_cq = done("p", g.iota(T.cq[:], [[16, 64]], TC * rank + CAP * (N - 1), 0, allow_small_or_imprecise_dtypes=True))
        need("y", MD, ZD)
    else:
        RCV, CNT, WD = [], ("cnt", N), list(weights())
        need("p", *WD)
        send([([base], off, "wd", T.wt[:], T.wt[:])])
    need("y", CNT, *RCV)
    SY.dma_start(T.cb[0:N, :], T.cland[:, 0:64, :]).then_inc(T.sem["cd"], 16)
    CD = ("cd", 16)

    F16, F15, F32 = (T.fb[:, 128 * j:128 * j + 128] for j in range(3))
    v_f16 = done("v", V.tensor_scalar(F16, T.fi[:], 4, None, Op.arith_shift_right))
    v_f15 = done("v", V.tensor_scalar(F15, T.fi[:], 15, None, Op.bitwise_and))
    v_wle = done("v", V.tensor_scalar(T.wle[:], T.fi[:], P0, -1.0, Op.is_le, Op.mult))
    need("v", v_f16)
    v_ws = done("v", V.tensor_scalar(T.wsame[:], F16, P16, None, Op.is_equal))
    v_wl = done("v", V.tensor_scalar(T.wlt[:], F16, P16, None, Op.is_gt))
    need("v", v_f15)
    done("v", V.tensor_scalar(T.selq[:], F15, P15, None, Op.is_equal))
    v_sb = done("v", V.tensor_scalar(T.selb[:], F15, P15, None, Op.is_equal))
    need("v", v_ws, v_wle)
    v_wn = done("v", V.tensor_tensor(T.wneg[:], T.wle[:], T.wsame[:], Op.mult))
    need("t", v_ac, v_wl)
    t_b = done("t", PE.matmul(T.ps2[:, 0:1], T.wlt[:], T.acc[:, 256:257], True, True))
    need("t", v_wn)
    PE.matmul(T.ps1[:, 0:256], T.wsame[:], T.acc[:, 1:257], True, False)
    t_r = done("t", PE.matmul(T.ps1[:, 0:256], T.wneg[:], T.eq[:, 0:256], False, True))
    need("t", v_sb, g_lc)
    PE.matmul(T.ps5[:, 0:128], T.selb[0:16, :], T.lc[0:16, :], True, False)
    need("v", t_r, t_b)
    need("v", done("v", V.tensor_scalar(T.rb[:], T.ps1[:, 0:256], T.ps2[:, 0:1], None, Op.add)))
    v_re = done("v", V.tensor_tensor(T.rbe[:], T.rb[:], T.eq[:, 0:256], Op.mult))
    need("t", v_re)
    for m in range(4):
        ins = PE.matmul(T.ps3[:, 0:64], T.selq[:], T.rbe[:, 64 * m:64 * m + 64], m == 0, m == 3)
    t_p = done("t", ins)
    v_xz = done("v", V.memset(T.xp[:, TC:], 0.0))
    need("v", t_p)
    need("v", done("v", V.tensor_copy(T.off1[:], T.ps3[:, 0:64])))

    def scatter(a, b, *toks):
        need("v", *toks)
        return done("v", V.tensor_copy(T.xp[:, 0:TC].indirect(T.off1[:, 8 * a:8 * b]), T.xs[:, cols(a, b - a)]))

    v_xp = scatter(0, 8, XD, XE) if isr else scatter(4, 8, scatter(0, 4, XD), XE)

    q0, m0 = rank // 4, rank % 4
    wq = lambda q: (T.wt[0:N, 12 * q:12 * q + 12], T.wt[0:N, 48 + 12 * q:60 + 12 * q])
    need("t", CD, *WD)
    PE.matmul(T.ps4[0:32, 0:12], T.cb[0:N, 0:32], wq(q0)[0], True, False)
    t_s = done("t", PE.matmul(T.ps4[0:32, 0:12], T.cb[0:N, 32:64], wq(q0)[1], False, True))
    need("v", t_s, g_d8)
    v_c1 = done("v", V.tensor_scalar(T.c1[0:32, :], T.d8[0:32, :], T.ps4[0:32, m0:m0 + 1], 0.0, Op.subtract, Op.max))
    need("v", v_c1)
    v_c2 = done("v", V.tensor_scalar(T.c2[0:32, :], T.c1[0:32, :], T.ps4[0:32, 4 + m0:5 + m0], None, Op.min))
    need("t", v_c2)
    t_l = done("t", PE.matmul(T.ps5[:, 0:128], T.onesb[0:32, 0:128], T.c2[0:32, :], False, True))
    need("v", t_l)
    v_o2 = done("v", V.tensor_copy(T.off2[:], T.ps5[:, 0:128]))

    def gather(qn, buf, lo, n=1):
        o, i = buf[:, CAP * lo:CAP * (lo + n)], T.xp[:].indirect(T.off2[:, 8 * lo:8 * (lo + n)])
        need(qn, v_o2, v_xp, v_xz)
        return done(qn, V.tensor_copy(o, i) if qn == "v" else SC.activation(o, i, Fn.Copy))

    mine, snd = T.land[:, cols(rank)], lambda c: T.snd[:, cols(rk(c))]
    a, b = MINE if isr else HIS
    near = chipmates[0:1] if isr else chipmates[1:]

    def two(cs):
        return [gather("v", T.snd, rk(cs[a])), gather("s", T.snd, rk(cs[b]))]

    need("p", *two(diag))
    send([([RELAY[rpeer][j]], first[j], "ra", snd(diag[j]), T.rela[:]) for j in (a, b)])
    need("p", *two(cabp))
    send([([cabp[j]], odd[2 * i:2 * i + 2], "dat", snd(cabp[j]), mine) for i, j in enumerate((a, b))])
    need("p", *two(rackp), *[gather("sv"[j], T.snd, rk(c)) for j, c in enumerate(near)])
    send([([rackp[j]], even[2 * i:2 * i + 2], "dat", snd(rackp[j]), mine) for i, j in enumerate((a, b))]
         + [([c], rest[2 * j:2 * j + 2], "dat", snd(c), mine) for j, c in enumerate(near)])
    if not isr:
        need("p", ("ls", left[0]))
        need("y", KD, XD, XE, CD, *[(q, made[q]) for q in made])
        return
    v_own = gather("v", T.land, rank)
    DAT = ("dat", 2 * (3 + 4 + 4) + 4 * len(off))

    HIF, LOF, DD = 0, 4, 8
    U4, V4, BD, JC, O4 = (T.tf[:, j:j + 4] for j in (12, 16, 20, 24, 28))
    BLK, NBLK, BLKS, BLK3 = (T.bk[:, 128 * j:128 * j + 128] for j in range(4))
    v_o4 = done("v", V.memset(O4, float(CAP)))
    v_of = done("v", V.memset(T.onef[:], 1.0))
    v_zz = done("v", V.memset(T.zz[:], 0.0))
    v_qf = done("v", V.tensor_copy(T.qf[:], F15))
    need("v", done("v", V.tensor_scalar(F32, T.fi[:], 5, None, Op.arith_shift_right)))
    done("v", V.tensor_scalar(BLK, F32, P32, None, Op.is_equal))
    done("v", V.tensor_scalar(NBLK, F32, P32, -1.0, Op.is_equal, Op.mult))
    done("v", V.tensor_scalar(BLKS, F32, P32n, None, Op.is_equal))
    need("v", v_of, done("v", V.tensor_scalar(T.kk[:, 5:6], P32, 3.0, -1.0, Op.is_equal, Op.mult)))
    v_b3 = done("v", V.tensor_scalar(BLK3, T.onef[:], T.kk[:, 5:6], None, Op.mult))
    need("v", g_cq)
    v_ci = done("v", V.tensor_scalar(T.ci[:], T.cq[:], P15, None, Op.add))

    need("p", v_o4)
    g_jc = done("p", g.affine_select(JC, O4, [[1000, 4]], Op.is_gt, float(-CAP * (N - 1)), -31, 1))
    for q in range(4):
        o = T.ps6[32 * q:32 * q + 32, 0:12]
        PE.matmul(o, T.cb[0:N, 0:32], wq(q)[0], True, False)
        t_y = done("t", PE.matmul(o, T.cb[0:N, 32:64], wq(q)[1], False, True))
    need("v", t_y, g_jc)
    v_ti = done("v", V.tensor_scalar(T.ti[:, 0:4], T.ps6[:, 0:4], float(TC * rank), None, Op.subtract))
    v_u = done("v", V.tensor_scalar(U4, T.ps6[:, 0:4], -1.0, float(TC * rank), Op.mult, Op.add))
    v_bd = done("v", V.tensor_tensor(BD, T.ps6[:, 8:12], JC, Op.add))
    need("v", v_u)
    need("v", done("v", V.tensor_scalar(V4, U4, 0.0, None, Op.max)), v_zz)
    v_z = done("v", V.tensor_tensor(T.zz[:, 1:5], V4, T.ps6[:, 4:8], Op.min))
    need("t", v_z, v_b3)
    PE.matmul(T.ps7[:, 0:4], NBLK, T.zz[:, 1:5], True, False)
    PE.matmul(T.ps7[:, 0:4], BLK, T.zz[:, 0:4], False, False)
    t_d = done("t", PE.matmul(T.ps7[:, 0:4], BLKS, T.zz[:, 4:8], False, True))
    t_15 = done("t", PE.matmul(T.ps2[:, 0:1], BLK3, T.zz[:, 4:5], True, True))
    need("v", v_ti)
    done("v", V.tensor_scalar(T.ti[:, 4:8], T.ti[:, 0:4], 4, None, Op.arith_shift_right))
    need("v", done("v", V.tensor_scalar(T.ti[:, 8:12], T.ti[:, 0:4], 15, None, Op.bitwise_and)))
    done("v", V.tensor_copy(T.tf[:, HIF:HIF + 8], T.ti[:, 4:12]))
    need("v", t_d, v_bd)
    v_dd = done("v", V.tensor_tensor(T.tf[:, DD:DD + 4], T.ps7[:, 0:4], BD, Op.add))
    need("v", v_dd, v_qf, g_cf)
    for m in range(4):
        hi, lo, jump = (T.tf[:, b_ + m:b_ + m + 1] for b_ in (HIF, LOF, DD))
        lm, r1, r2 = T.lm[:, 128 * m:128 * m + 128], T.r1[:, 64 * m:64 * m + 64], T.r2[:, 64 * m:64 * m + 64]
        done("v", V.tensor_scalar(lm, T.qf[:], lo, None, Op.is_ge))
        done("v", V.tensor_scalar(r1, T.cf[:], hi, jump, Op.is_equal, Op.mult))
        need("t", done("v", V.tensor_scalar(r2, T.cf[:], hi, jump, Op.is_gt, Op.mult)))
        PE.matmul(T.ps1[:, 0:64], lm, r1, m == 0, False)
        ins = PE.matmul(T.ps1[:, 0:64], T.onef[:], r2, False, m == 3)
    t_w = done("t", ins)
    need("v", t_w, v_ci)
    need("v", done("v", V.tensor_tensor(T.w1[:], T.ps1[:, 0:64], T.ci[:], Op.add)), t_15)
    v_o3 = done("v", V.tensor_scalar(T.off3[:], T.w1[:], T.ps2[:, 0:1], None, Op.add))

    tok = {}
    for j in (0, 2, 1, 3):
        w, i = slice(256 * j, 256 * j + 256), T.land[:].indirect(T.off3[:, 16 * j:16 * j + 16])
        qn = "v" if j < 2 else "s"
        need(qn, v_o3, v_own, DAT)
        tok[j] = done(qn, V.tensor_copy(T.yb[:, w], i) if j < 2 else SC.activation(T.yb[:, w], i, Fn.Copy))
    for j, qn in ((0, "y"), (2, "y"), (1, "y"), (3, "s")):
        w = slice(256 * j, 256 * j + 256)
        need(qn, tok[j])
        queue[qn].dma_start(T.y[:, w], T.yb[:, w]).then_inc(T.sem["yd"], 16)

    need("p", ("ls", left[0]))
    need("y", KD, XD, XE, MD, ZD, CD, *WD, ("yd", 64), *[(q, made[q]) for q in made])
